import numpy as np
import ml_dtypes


def mxq(x, axis, fmt="e4m3"):
    dtype, down = {"e4m3": (ml_dtypes.float8_e4m3fn, 7), "e5m2": (ml_dtypes.float8_e5m2, 14)}[fmt]
    v = np.moveaxis(np.asarray(x, np.float32).astype(ml_dtypes.bfloat16).astype(np.float64), axis, -1)
    blocks = v.reshape(v.shape[:-1] + (-1, 32))
    amax = np.abs(blocks).max(-1, keepdims=True)
    byte = np.maximum(np.where(amax > 0, np.frexp(amax)[1] - 1 + 127, 0) - down, 1)
    scale = np.exp2(byte - 127.0)
    codes = (blocks / scale).astype(np.float32).astype(dtype).astype(np.float64)
    return np.moveaxis((codes * scale).reshape(v.shape), -1, axis)


WIDE = False


def mx_kscale(k):
    if not WIDE:
        return np.ones(k)
    levels = np.array([10, -10, 5, -5, 0])
    if k % 512:
        return np.exp2(np.random.permutation(np.resize(levels, k // 32))).repeat(32)
    a = np.empty((k // 512, 16))
    for p in range(k // 512):
        a[p, :8] = np.random.permutation(np.resize(levels, 8))
        for g in range(8):
            far = levels[np.abs(levels - a[p, g]) >= 10]
            a[p, g + 8] = far[np.random.randint(len(far))]
    return np.exp2(a.ravel()).repeat(32)


def f64(x):
    return np.asarray(x).astype(np.float64)


def striped(idx):
    return np.tile(idx.reshape(-1, 16).T, (8, 1)).astype(np.uint16)


def unstriped(offs):
    return offs[:16].T.reshape(-1).astype(np.int64)


def pack_weight(w):
    k, n = w.shape
    w = f64(np.asarray(w, np.float32).astype(ml_dtypes.bfloat16)).reshape(k // 32, 32, n)
    amax = np.abs(w).max(1)
    byte = np.clip(np.where(amax > 0, np.frexp(amax)[1] - 1 + 127 - 7, 1), 1, 254)
    scaled = (w * np.exp2(127.0 - byte)[:, None, :]).reshape(k, n).astype(np.float32)
    words = np.ascontiguousarray(scaled.reshape(k // 512, 128, 4, n).transpose(0, 1, 3, 2)).astype(ml_dtypes.float8_e4m3fn).view(np.uint8)
    return words, np.ascontiguousarray(byte.astype(np.uint8).reshape(k // 512, 16, n))


def unpack_weight(words, scales):
    g, p, n, _ = words.shape
    vals = np.ascontiguousarray(words).view(ml_dtypes.float8_e4m3fn).astype(np.float64) * np.repeat(np.exp2(scales.astype(np.float64) - 127.0), 8, axis=1)[..., None]
    return vals.transpose(0, 1, 3, 2).reshape(g * 512, n)


def silu(v):
    return v / (1.0 + np.exp(-np.maximum(v, -700.0)))


K, T, D, S, V, H, N = 512, 2048, 3, 512, 256, 512, 512
P = 2 ** 7


def setup_inputs():
    n = np.random.standard_normal
    s = mx_kscale(K)[:, None]
    u = mx_kscale(H)
    q = np.random.permutation(S)
    packed = pack_weight(n((K, T)) * s)
    return {
        "x_words": packed[0],
        "x_scales": packed[1],
        "w1": (n((K, H)) / np.sqrt(K) / s * u).astype(np.float32),
        "w2": (n((H, N)) / np.sqrt(H) / u[:, None]).astype(np.float32),
        "gate": np.tile(np.random.uniform(0.2, 1.0, (D, 1, V)) / np.sqrt(D), (1, P, 1)).astype(np.float32),
        "offs": striped(np.random.permutation(T)[:S]),
        "pos1": striped(q[:V]),
        "pos2": striped(q[V:]),
        "pos3": striped(np.random.permutation(S)[:V]),
    }


def reference(x_words, x_scales, w1, w2, gate, offs, pos1, pos2, pos3):
    h = silu(mxq(f64(w1), 0, "e4m3").T @ unpack_weight(x_words, x_scales)[:, unstriped(offs)])
    z = sum(f64(gate)[d, :1] * h[:, unstriped(p)] for d, p in enumerate((pos1, pos2, pos3)))
    return mxq(f64(w2), 0, "e4m3").T @ mxq(z, 0, "e4m3")

@@ -1,0 +1,169 @@
+from contextlib import ExitStack
+
+import concourse.mybir as mybir
+from concourse.masks import make_identity
+
+K, T, D, S, V, H, N = 512, 2048, 3, 512, 256, 512, 512
+FLOPS = 2 * K * H * S + 2 * H * N * V
+
+F32 = mybir.dt.float32
+BF16 = mybir.dt.bfloat16
+I32 = mybir.dt.int32
+U32 = mybir.dt.uint32
+U16 = mybir.dt.uint16
+U8 = mybir.dt.uint8
+FP8X4 = mybir.dt.float8_e4m3fn_x4
+MULT = mybir.AluOpType.mult
+SILU = mybir.ActivationFunctionType.Silu
+P = 128
+
+
+def interleave(copy, grouped, raw):
+    copy(grouped.rearrange("p (c i) j -> p c j i", i=4), raw.rearrange("p j (c i) -> p c j i", i=4))
+
+
+def tile_picked_sage_silu_p_kernel(tc, x_words, x_scales, w1, w2, gate, offs, pos1, pos2, pos3, out):
+    nc = tc.nc
+    with ExitStack() as ctx:
+        keep = ctx.enter_context(tc.tile_pool(name="keep", bufs=1))
+        psum = ctx.enter_context(tc.psum_pool(name="psum", bufs=1))
+
+        def sb(shape, dtype, name, tag=None):
+            return keep.tile(shape, dtype, name=name, tag=tag or name, align_bytes=64)
+
+        def bank(b, shape, name):
+            return psum.tile(shape, F32, name=name, tag="bank%d" % b)
+
+        offs_t = sb([P, S // 16], U16, "offs_t")
+        pos_t = [sb([P, V // 16], U16, "pos_t%d" % d) for d in range(D)]
+        xw = sb([P, T], I32, "xw")
+        xs = sb([P, T], U8, "xs")
+        w1_raw = [sb([P, 4, 128], F32, "w1_raw%d" % c) for c in range(4)]
+        w2_raw = [sb([P, 4, 256], F32, "w2_raw%d" % a) for a in range(2)]
+        gate0 = sb([P, V], F32, "gate0")
+        gate12 = sb([P, 2, V], F32, "gate12")
+        gate_t = [gate0[:], gate12[:, 0, :], gate12[:, 1, :]]
+        ident = sb([P, P], F32, "ident")
+
+        w1_v = w1.rearrange("(p j) c -> p j c", j=4)
+        w2_v = w2.rearrange("(p j) c -> p j c", j=4)
+
+        nc.gpsimd.memset(xs[:].bitcast(I32), 0)
+        nc.sync.dma_start(offs_t[:], offs)
+        nc.sync.dma_start(w1_raw[0][:], w1_v[:, :, 0:128])
+        nc.sync.dma_start(pos_t[0][:], pos1)
+        nc.sync.dma_start(xw[:], x_words[0].rearrange("p n t -> p (n t)").bitcast(I32))
+        for q in range(4):
+            nc.scalar.dma_start(xs[32 * q : 32 * q + 4, :].bitcast(I32), x_scales[0, 4 * q : 4 * q + 4, :].bitcast(I32))
+        nc.sync.dma_start(w1_raw[1][:], w1_v[:, :, 128:256])
+        nc.sync.dma_start(gate0[:], gate[0])
+        nc.sync.dma_start(w1_raw[2][:], w1_v[:, :, 256:384])
+        nc.sync.dma_start(pos_t[1][:], pos2)
+        nc.sync.dma_start(gate12[:], gate[1:3].rearrange("d p v -> p d v"))
+        nc.sync.dma_start(pos_t[2][:], pos3)
+        nc.sync.dma_start(w1_raw[3][:], w1_v[:, :, 384:512])
+        for a in range(2):
+            nc.sync.dma_start(w2_raw[a][:], w2_v[:, :, 256 * a : 256 * (a + 1)])
+        make_identity(nc, ident[:])
+
+        def quantised(copy, raw, name):
+            grouped = sb([P, 128, 4], BF16, name + "_g")
+            codes = sb([P, 128], U32, name + "_c")
+            scales = sb([P, 128], U8, name + "_s")
+            interleave(copy, grouped[:], raw)
+            nc.vector.quantize_mx(codes[:].bitcast(FP8X4), scales[:], grouped[:].rearrange("p c j -> p (c j)"))
+            return codes, scales
+
+        w1_src = [w1_raw[c][:] for c in range(4)]
+        w2_src = [w2_raw[m // 2][:, :, 128 * (m % 2) : 128 * (m % 2 + 1)] for m in range(4)]
+
+        xg = sb([P, S], U32, "xg")
+        sg = sb([P, S], U8, "sg")
+        h = {}
+
+        def first_layer(c, wq, a, b, bk):
+            acc = bank(bk, [P, b - a], "acc%d_%d" % (c, a))
+            nc.tensor.matmul_mx(acc[:], lhsT=wq[0][:].bitcast(FP8X4), lhsT_scale=wq[1][:],
+                                rhs=xg[:, a:b].bitcast(FP8X4), rhs_scale=sg[:, a:b], start=True, stop=True)
+            nc.scalar.activation(h[c][:, a:b], acc[:], SILU)
+
+        h[0] = sb([P, S], F32, "h0")
+        wq0 = quantised(nc.vector.tensor_copy, w1_src[0], "w1q0")
+        nc.vector.tensor_copy(sg[:], xs[:].indirect(offs_t[:]))
+        for half in range(2):
+            a, b = 256 * half, 256 * (half + 1)
+            nc.vector.tensor_copy(xg[:, a:b], xw[:].bitcast(U32).indirect(offs_t[:, a // 16 : b // 16]))
+            first_layer(0, wq0, a, b, half)
+        wq1 = quantised(nc.vector.tensor_copy, w1_src[1], "w1q1")
+        wq2 = quantised(nc.scalar.copy, w1_src[2], "w1q2")
+        h[1] = sb([P, S], F32, "h1", tag="w1_raw2")
+        first_layer(1, wq1, 0, S, 2)
+        wq3 = quantised(nc.scalar.copy, w1_src[3], "w1q3")
+        h[2] = sb([P, S], F32, "h2")
+        first_layer(2, wq2, 0, S, 0)
+        h[3] = sb([P, S], F32, "h3")
+        first_layer(3, wq3, 0, S, 1)
+
+        w2g = sb([P, N, 4], BF16, "w2g")
+        w2c = sb([P, N], U32, "w2c")
+        w2s = sb([P, N], U8, "w2s")
+        for m in range(4):
+            interleave(nc.scalar.copy, w2g[:, 128 * m : 128 * (m + 1), :], w2_src[m])
+
+        def neighbours(c, vbs, dst):
+            a, b = 128 * vbs[0], 128 * (vbs[-1] + 1)
+            for d in range(D):
+                g = sb([P, b - a], F32, "g%d_%d_%d" % (c, a, d))
+                nc.vector.tensor_tensor(g[:], h[c][:].indirect(pos_t[d][:, a // 16 : b // 16]), gate_t[d][:, a:b], MULT)
+                for vb in vbs:
+                    nc.tensor.matmul(dst[vb], lhsT=g[:, 128 * vb - a : 128 * (vb + 1) - a], rhs=ident[:],
+                                     start=(d == 0), stop=(d == D - 1), is_transpose=True)
+
+        def round_z(zt, src, p0, p1):
+            nc.scalar.copy(zt[:].rearrange("v (u p e) -> v u p e", u=2, e=2)[:, :, p0:p1, :],
+                           src.rearrange("v (p u e) -> v u p e", u=2, e=2))
+
+        def turn_back(vb, zt, bk):
+            back = bank(bk, [P, 2, 128], "back%d" % vb)
+            words = zt[:].bitcast(F32)
+            for u in range(2):
+                nc.tensor.transpose(back[:, u, :], words[:, 128 * u : 128 * (u + 1)], ident[:])
+            zg = sb([P, 512], BF16, "zg%d" % vb)
+            nc.scalar.copy(zg[:].bitcast(F32).rearrange("p (v u) -> p v u", u=2), back[:].rearrange("p u v -> p v u"))
+            return zg
+
+        def second_layer(vb, zg, parts):
+            zc = sb([P, 128], U32, "zc%d" % vb)
+            zs = sb([P, 128], U8, "zs%d" % vb)
+            nc.vector.quantize_mx(zc[:].bitcast(FP8X4), zs[:], zg[:])
+            for m0, m1, bk, copy in parts:
+                acc = bank(bk, [P, m1 - m0, 128], "out%d_%d" % (vb, m0))
+                for m in range(m0, m1):
+                    cols = slice(128 * m, 128 * (m + 1))
+                    nc.tensor.matmul_mx(acc[:, m - m0, :], lhsT=w2c[:, cols].bitcast(FP8X4), lhsT_scale=w2s[:, cols],
+                                        rhs=zc[:].bitcast(FP8X4), rhs_scale=zs[:], start=True, stop=True)
+                res = sb([P, m1 - m0, 128], F32, "res%d_%d" % (vb, m0))
+                rows = out[128 * m0 : 128 * m1, 128 * vb : 128 * (vb + 1)].rearrange("(j p) v -> p j v", p=P)
+                copy(res[:], acc[:])
+                nc.sync.dma_start(rows, res[:])
+
+        early = [bank(3 + vb, [P, 384], "early%d" % vb) for vb in range(2)]
+        for c in range(2):
+            neighbours(c, [0, 1], [early[vb][:, 128 * c : 128 * (c + 1)] for vb in range(2)])
+        neighbours(2, [0], {0: early[0][:, 256:384]})
+        zt0 = sb([P, H], BF16, "zt0", tag="w2_raw1")
+        round_z(zt0, early[0][:], 0, 96)
+        late0 = bank(5, [P, 128], "late0")
+        neighbours(3, [0], {0: late0[:]})
+        round_z(zt0, late0[:], 96, 128)
+        zg0 = turn_back(0, zt0, 6)
+        neighbours(2, [1], {1: early[1][:, 256:384]})
+        zt1 = sb([P, H], BF16, "zt1")
+        round_z(zt1, early[1][:], 0, 96)
+        late1 = bank(6, [P, 128], "late1")
+        neighbours(3, [1], {1: late1[:]})
+        round_z(zt1, late1[:], 96, 128)
+        zg1 = turn_back(1, zt1, 7)
+        nc.vector.quantize_mx(w2c[:].bitcast(FP8X4), w2s[:], w2g[:].rearrange("p c j -> p (c j)"))
+        second_layer(0, zg0, [(0, 4, 6, nc.scalar.copy)])
+        second_layer(1, zg1, [(0, 2, 0, nc.vector.tensor_copy), (2, 4, 1, nc.scalar.copy)])

@@ -19,7 +19,7 @@ P = 128
 
 
 def interleave(copy, grouped, raw):
-    copy(grouped.rearrange("p (c i) j -> p c j i", i=4), raw.rearrange("p j (c i) -> p c j i", i=4))
+    copy(grouped, raw.rearrange("p j c -> p c j"))
 
 
 def tile_picked_sage_silu_p_kernel(tc, x_words, x_scales, w1, w2, gate, offs, pos1, pos2, pos3, out):
@@ -38,8 +38,9 @@ def tile_picked_sage_silu_p_kernel(tc, x_words, x_scales, w1, w2, gate, offs, po
         pos_t = [sb([P, V // 16], U16, "pos_t%d" % d) for d in range(D)]
         xw = sb([P, T], I32, "xw")
         xs = sb([P, T], U8, "xs")
-        w1_raw = [sb([P, 4, 128], F32, "w1_raw%d" % c) for c in range(4)]
-        w2_raw = [sb([P, 4, 256], F32, "w2_raw%d" % a) for a in range(2)]
+        w1_cols = [(0, 128), (128, 384), (384, 512)]
+        w1_raw = [sb([P, 4, b - a], F32, "w1_raw%d" % a) for a, b in w1_cols]
+        w2_raw = sb([P, 4, N], F32, "w2_raw")
         gate0 = sb([P, V], F32, "gate0")
         gate12 = sb([P, 2, V], F32, "gate12")
         gate_t = [gate0[:], gate12[:, 0, :], gate12[:, 1, :]]
@@ -48,22 +49,20 @@ def tile_picked_sage_silu_p_kernel(tc, x_words, x_scales, w1, w2, gate, offs, po
         w1_v = w1.rearrange("(p j) c -> p j c", j=4)
         w2_v = w2.rearrange("(p j) c -> p j c", j=4)
 
-        nc.gpsimd.memset(xs[:].bitcast(I32), 0)
+        nc.vector.memset(xs[:].bitcast(I32), 0)
         nc.sync.dma_start(offs_t[:], offs)
         nc.sync.dma_start(w1_raw[0][:], w1_v[:, :, 0:128])
-        nc.sync.dma_start(pos_t[0][:], pos1)
-        nc.sync.dma_start(xw[:], x_words[0].rearrange("p n t -> p (n t)").bitcast(I32))
         for q in range(4):
-            nc.scalar.dma_start(xs[32 * q : 32 * q + 4, :].bitcast(I32), x_scales[0, 4 * q : 4 * q + 4, :].bitcast(I32))
-        nc.sync.dma_start(w1_raw[1][:], w1_v[:, :, 128:256])
+            nc.sync.dma_start(xs[32 * q : 32 * q + 4, :].bitcast(I32), x_scales[0, 4 * q : 4 * q + 4, :].bitcast(I32))
+        nc.sync.dma_start(xw[:], x_words[0].rearrange("p n t -> p (n t)").bitcast(I32))
+        nc.sync.dma_start(w1_raw[1][:], w1_v[:, :, 128:384])
+        nc.sync.dma_start(pos_t[0][:], pos1)
         nc.sync.dma_start(gate0[:], gate[0])
-        nc.sync.dma_start(w1_raw[2][:], w1_v[:, :, 256:384])
         nc.sync.dma_start(pos_t[1][:], pos2)
         nc.sync.dma_start(gate12[:], gate[1:3].rearrange("d p v -> p d v"))
         nc.sync.dma_start(pos_t[2][:], pos3)
-        nc.sync.dma_start(w1_raw[3][:], w1_v[:, :, 384:512])
-        for a in range(2):
-            nc.sync.dma_start(w2_raw[a][:], w2_v[:, :, 256 * a : 256 * (a + 1)])
+        nc.sync.dma_start(w1_raw[2][:], w1_v[:, :, 384:512])
+        nc.sync.dma_start(w2_raw[:], w2_v)
         make_identity(nc, ident[:])
 
         def quantised(copy, raw, name):
@@ -74,8 +73,8 @@ def tile_picked_sage_silu_p_kernel(tc, x_words, x_scales, w1, w2, gate, offs, po
             nc.vector.quantize_mx(codes[:].bitcast(FP8X4), scales[:], grouped[:].rearrange("p c j -> p (c j)"))
             return codes, scales
 
-        w1_src = [w1_raw[c][:] for c in range(4)]
-        w2_src = [w2_raw[m // 2][:, :, 128 * (m % 2) : 128 * (m % 2 + 1)] for m in range(4)]
+        w1_src = [w1_raw[0][:], w1_raw[1][:, :, 0:128], w1_raw[1][:, :, 128:256], w1_raw[2][:]]
+        w2_src = [w2_raw[:, :, 128 * m : 128 * (m + 1)] for m in range(4)]
 
         xg = sb([P, S], U32, "xg")
         sg = sb([P, S], U8, "sg")
@@ -94,11 +93,11 @@ def tile_picked_sage_silu_p_kernel(tc, x_words, x_scales, w1, w2, gate, offs, po
             a, b = 256 * half, 256 * (half + 1)
             nc.vector.tensor_copy(xg[:, a:b], xw[:].bitcast(U32).indirect(offs_t[:, a // 16 : b // 16]))
             first_layer(0, wq0, a, b, half)
-        wq1 = quantised(nc.vector.tensor_copy, w1_src[1], "w1q1")
-        wq2 = quantised(nc.scalar.copy, w1_src[2], "w1q2")
-        h[1] = sb([P, S], F32, "h1", tag="w1_raw2")
-        first_layer(1, wq1, 0, S, 2)
+        wq1 = quantised(nc.scalar.copy, w1_src[1], "w1q1")
+        wq2 = quantised(nc.vector.tensor_copy, w1_src[2], "w1q2")
         wq3 = quantised(nc.scalar.copy, w1_src[3], "w1q3")
+        h[1] = sb([P, S], F32, "h1", tag="w1_raw384")
+        first_layer(1, wq1, 0, S, 2)
         h[2] = sb([P, S], F32, "h2")
         first_layer(2, wq2, 0, S, 0)
         h[3] = sb([P, S], F32, "h3")
@@ -148,21 +147,19 @@ def tile_picked_sage_silu_p_kernel(tc, x_words, x_scales, w1, w2, gate, offs, po
                 nc.sync.dma_start(rows, res[:])
 
         early = [bank(3 + vb, [P, 384], "early%d" % vb) for vb in range(2)]
-        for c in range(2):
+        for c in range(3):
             neighbours(c, [0, 1], [early[vb][:, 128 * c : 128 * (c + 1)] for vb in range(2)])
-        neighbours(2, [0], {0: early[0][:, 256:384]})
-        zt0 = sb([P, H], BF16, "zt0", tag="w2_raw1")
+        zt0 = sb([P, H], BF16, "zt0", tag="w2_raw")
         round_z(zt0, early[0][:], 0, 96)
+        zt1 = sb([P, H], BF16, "zt1")
+        round_z(zt1, early[1][:], 0, 96)
         late0 = bank(5, [P, 128], "late0")
         neighbours(3, [0], {0: late0[:]})
         round_z(zt0, late0[:], 96, 128)
-        zg0 = turn_back(0, zt0, 6)
-        neighbours(2, [1], {1: early[1][:, 256:384]})
-        zt1 = sb([P, H], BF16, "zt1")
-        round_z(zt1, early[1][:], 0, 96)
         late1 = bank(6, [P, 128], "late1")
         neighbours(3, [1], {1: late1[:]})
         round_z(zt1, late1[:], 96, 128)
+        zg0 = turn_back(0, zt0, 2)
         zg1 = turn_back(1, zt1, 7)
         nc.vector.quantize_mx(w2c[:].bitcast(FP8X4), w2s[:], w2g[:].rearrange("p c j -> p (c j)"))
         second_layer(0, zg0, [(0, 4, 6, nc.scalar.copy)])

@@ -38,7 +38,7 @@ def tile_picked_sage_silu_p_kernel(tc, x_words, x_scales, w1, w2, gate, offs, po
         pos_t = [sb([P, V // 16], U16, "pos_t%d" % d) for d in range(D)]
         xw = sb([P, T], I32, "xw")
         xs = sb([P, T], U8, "xs")
-        w1_cols = [(0, 128), (128, 384), (384, 512)]
+        w1_cols = [(0, 128), (128, 256), (256, 512)]
         w1_raw = [sb([P, 4, b - a], F32, "w1_raw%d" % a) for a, b in w1_cols]
         w2_raw = sb([P, 4, N], F32, "w2_raw")
         gate0 = sb([P, V], F32, "gate0")
@@ -50,18 +50,23 @@ def tile_picked_sage_silu_p_kernel(tc, x_words, x_scales, w1, w2, gate, offs, po
         w2_v = w2.rearrange("(p j) c -> p j c", j=4)
 
         nc.vector.memset(xs[:].bitcast(I32), 0)
+        warm = sb([P, 2], F32, "warm")
+        nc.vector.memset(warm[:, 0:1], 0.0)
+        nc.scalar.activation(warm[:, 1:2], warm[:, 0:1], SILU)
         nc.sync.dma_start(offs_t[:], offs)
-        nc.sync.dma_start(w1_raw[0][:], w1_v[:, :, 0:128])
+        words_in = x_words[0].rearrange("p n t -> p (n t)").bitcast(I32)
+        nc.sync.dma_start(xw[:, 0 : T // 2], words_in[:, 0 : T // 2])
         for q in range(4):
             nc.sync.dma_start(xs[32 * q : 32 * q + 4, :].bitcast(I32), x_scales[0, 4 * q : 4 * q + 4, :].bitcast(I32))
-        nc.sync.dma_start(xw[:], x_words[0].rearrange("p n t -> p (n t)").bitcast(I32))
-        nc.sync.dma_start(w1_raw[1][:], w1_v[:, :, 128:384])
+        nc.sync.dma_start(w1_raw[0][:], w1_v[:, :, 0:128])
+        nc.sync.dma_start(xw[:, T // 2 : T], words_in[:, T // 2 : T])
+        nc.sync.dma_start(w1_raw[1][:], w1_v[:, :, 128:256])
         nc.sync.dma_start(pos_t[0][:], pos1)
         nc.sync.dma_start(gate0[:], gate[0])
         nc.sync.dma_start(pos_t[1][:], pos2)
         nc.sync.dma_start(gate12[:], gate[1:3].rearrange("d p v -> p d v"))
         nc.sync.dma_start(pos_t[2][:], pos3)
-        nc.sync.dma_start(w1_raw[2][:], w1_v[:, :, 384:512])
+        nc.sync.dma_start(w1_raw[2][:], w1_v[:, :, 256:512])
         nc.sync.dma_start(w2_raw[:], w2_v)
         make_identity(nc, ident[:])
 
@@ -73,7 +78,7 @@ def tile_picked_sage_silu_p_kernel(tc, x_words, x_scales, w1, w2, gate, offs, po
             nc.vector.quantize_mx(codes[:].bitcast(FP8X4), scales[:], grouped[:].rearrange("p c j -> p (c j)"))
             return codes, scales
 
-        w1_src = [w1_raw[0][:], w1_raw[1][:, :, 0:128], w1_raw[1][:, :, 128:256], w1_raw[2][:]]
+        w1_src = [w1_raw[0][:], w1_raw[1][:], w1_raw[2][:, :, 0:128], w1_raw[2][:, :, 128:256]]
         w2_src = [w2_raw[:, :, 128 * m : 128 * (m + 1)] for m in range(4)]
 
         xg = sb([P, S], U32, "xg")
@@ -87,16 +92,20 @@ def tile_picked_sage_silu_p_kernel(tc, x_words, x_scales, w1, w2, gate, offs, po
             nc.scalar.activation(h[c][:, a:b], acc[:], SILU)
 
         h[0] = sb([P, S], F32, "h0")
-        wq0 = quantised(nc.vector.tensor_copy, w1_src[0], "w1q0")
+        wq0 = quantised(nc.scalar.copy, w1_src[0], "w1q0")
         nc.vector.tensor_copy(sg[:], xs[:].indirect(offs_t[:]))
         for half in range(2):
             a, b = 256 * half, 256 * (half + 1)
             nc.vector.tensor_copy(xg[:, a:b], xw[:].bitcast(U32).indirect(offs_t[:, a // 16 : b // 16]))
-            first_layer(0, wq0, a, b, half)
-        wq1 = quantised(nc.scalar.copy, w1_src[1], "w1q1")
-        wq2 = quantised(nc.vector.tensor_copy, w1_src[2], "w1q2")
+            if half == 0:
+                first_layer(0, wq0, a, b, 0)
+            else:
+                first_layer(0, wq0, a, a + 128, 1)
+                first_layer(0, wq0, a + 128, b, 7)
+        wq1 = quantised(nc.vector.tensor_copy, w1_src[1], "w1q1")
+        wq2 = quantised(nc.scalar.copy, w1_src[2], "w1q2")
         wq3 = quantised(nc.scalar.copy, w1_src[3], "w1q3")
-        h[1] = sb([P, S], F32, "h1", tag="w1_raw384")
+        h[1] = sb([P, S], F32, "h1", tag="w1_raw256")
         first_layer(1, wq1, 0, S, 2)
         h[2] = sb([P, S], F32, "h2")
         first_layer(2, wq2, 0, S, 0)
@@ -112,7 +121,7 @@ def tile_picked_sage_silu_p_kernel(tc, x_words, x_scales, w1, w2, gate, offs, po
         def neighbours(c, vbs, dst):
             a, b = 128 * vbs[0], 128 * (vbs[-1] + 1)
             for d in range(D):
-                g = sb([P, b - a], F32, "g%d_%d_%d" % (c, a, d))
+                g = sb([P, b - a], F32, "g%d_%d_%d" % (c, a, d), tag="w1q1_g" if (c, d) == (0, 0) else None)
                 nc.vector.tensor_tensor(g[:], h[c][:].indirect(pos_t[d][:, a // 16 : b // 16]), gate_t[d][:, a:b], MULT)
                 for vb in vbs:
                     nc.tensor.matmul(dst[vb], lhsT=g[:, 128 * vb - a : 128 * (vb + 1) - a], rhs=ident[:],
@@ -162,5 +171,5 @@ def tile_picked_sage_silu_p_kernel(tc, x_words, x_scales, w1, w2, gate, offs, po
         zg0 = turn_back(0, zt0, 2)
         zg1 = turn_back(1, zt1, 7)
         nc.vector.quantize_mx(w2c[:].bitcast(FP8X4), w2s[:], w2g[:].rearrange("p c j -> p (c j)"))
-        second_layer(0, zg0, [(0, 4, 6, nc.scalar.copy)])
+        second_layer(0, zg0, [(0, 2, 6, nc.scalar.copy), (2, 4, 3, nc.scalar.copy)])
         second_layer(1, zg1, [(0, 2, 0, nc.vector.tensor_copy), (2, 4, 1, nc.scalar.copy)])

@@ -19,7 +19,7 @@ P = 128
 
 
 def interleave(copy, grouped, raw):
-    copy(grouped, raw.rearrange("p j c -> p c j"))
+    copy(grouped.rearrange("p (c i) j -> p c j i", i=4), raw.rearrange("p j (c i) -> p c j i", i=4))
 
 
 def tile_picked_sage_silu_p_kernel(tc, x_words, x_scales, w1, w2, gate, offs, pos1, pos2, pos3, out):

from contextlib import ExitStack

import concourse.mybir as mybir
from concourse.masks import make_identity

K, T, D, S, V, H, N = 512, 2048, 3, 512, 256, 512, 512
FLOPS = 2 * K * H * S + 2 * H * N * V

F32 = mybir.dt.float32
BF16 = mybir.dt.bfloat16
I32 = mybir.dt.int32
U32 = mybir.dt.uint32
U16 = mybir.dt.uint16
U8 = mybir.dt.uint8
FP8X4 = mybir.dt.float8_e4m3fn_x4
MULT = mybir.AluOpType.mult
SILU = mybir.ActivationFunctionType.Silu
P = 128


def interleave(copy, grouped, raw):
    copy(grouped.rearrange("p (c i) j -> p c j i", i=4), raw.rearrange("p j (c i) -> p c j i", i=4))


def tile_picked_sage_silu_p_kernel(tc, x_words, x_scales, w1, w2, gate, offs, pos1, pos2, pos3, out):
    nc = tc.nc
    with ExitStack() as ctx:
        keep = ctx.enter_context(tc.tile_pool(name="keep", bufs=1))
        psum = ctx.enter_context(tc.psum_pool(name="psum", bufs=1))

        def sb(shape, dtype, name, tag=None):
            return keep.tile(shape, dtype, name=name, tag=tag or name, align_bytes=64)

        def bank(b, shape, name):
            return psum.tile(shape, F32, name=name, tag="bank%d" % b)

        offs_t = sb([P, S // 16], U16, "offs_t")
        pos_t = [sb([P, V // 16], U16, "pos_t%d" % d) for d in range(D)]
        xw = sb([P, T], I32, "xw")
        xs = sb([P, T], U8, "xs")
        w1_cols = [(0, 128), (128, 256), (256, 512)]
        w1_raw = [sb([P, 4, b - a], F32, "w1_raw%d" % a) for a, b in w1_cols]
        w2_raw = sb([P, 4, N], F32, "w2_raw")
        gate0 = sb([P, V], F32, "gate0")
        gate12 = sb([P, 2, V], F32, "gate12")
        gate_t = [gate0[:], gate12[:, 0, :], gate12[:, 1, :]]
        ident = sb([P, P], F32, "ident")

        w1_v = w1.rearrange("(p j) c -> p j c", j=4)
        w2_v = w2.rearrange("(p j) c -> p j c", j=4)

        nc.vector.memset(xs[:].bitcast(I32), 0)
        warm = sb([P, 2], F32, "warm")
        nc.vector.memset(warm[:, 0:1], 0.0)
        nc.scalar.activation(warm[:, 1:2], warm[:, 0:1], SILU)
        nc.sync.dma_start(offs_t[:], offs)
        words_in = x_words[0].rearrange("p n t -> p (n t)").bitcast(I32)
        nc.sync.dma_start(xw[:, 0 : T // 2], words_in[:, 0 : T // 2])
        for q in range(4):
            nc.sync.dma_start(xs[32 * q : 32 * q + 4, :].bitcast(I32), x_scales[0, 4 * q : 4 * q + 4, :].bitcast(I32))
        nc.sync.dma_start(w1_raw[0][:], w1_v[:, :, 0:128])
        nc.sync.dma_start(xw[:, T // 2 : T], words_in[:, T // 2 : T])
        nc.sync.dma_start(w1_raw[1][:], w1_v[:, :, 128:256])
        nc.sync.dma_start(pos_t[0][:], pos1)
        nc.sync.dma_start(gate0[:], gate[0])
        nc.sync.dma_start(pos_t[1][:], pos2)
        nc.sync.dma_start(gate12[:], gate[1:3].rearrange("d p v -> p d v"))
        nc.sync.dma_start(pos_t[2][:], pos3)
        nc.sync.dma_start(w1_raw[2][:], w1_v[:, :, 256:512])
        nc.sync.dma_start(w2_raw[:], w2_v)
        make_identity(nc, ident[:])

        def quantised(copy, raw, name):
            grouped = sb([P, 128, 4], BF16, name + "_g")
            codes = sb([P, 128], U32, name + "_c")
            scales = sb([P, 128], U8, name + "_s")
            interleave(copy, grouped[:], raw)
            nc.vector.quantize_mx(codes[:].bitcast(FP8X4), scales[:], grouped[:].rearrange("p c j -> p (c j)"))
            return codes, scales

        w1_src = [w1_raw[0][:], w1_raw[1][:], w1_raw[2][:, :, 0:128], w1_raw[2][:, :, 128:256]]
        w2_src = [w2_raw[:, :, 128 * m : 128 * (m + 1)] for m in range(4)]

        xg = sb([P, S], U32, "xg")
        sg = sb([P, S], U8, "sg")
        h = {}

        def first_layer(c, wq, a, b, bk):
            acc = bank(bk, [P, b - a], "acc%d_%d" % (c, a))
            nc.tensor.matmul_mx(acc[:], lhsT=wq[0][:].bitcast(FP8X4), lhsT_scale=wq[1][:],
                                rhs=xg[:, a:b].bitcast(FP8X4), rhs_scale=sg[:, a:b], start=True, stop=True)
            nc.scalar.activation(h[c][:, a:b], acc[:], SILU)

        h[0] = sb([P, S], F32, "h0")
        wq0 = quantised(nc.scalar.copy, w1_src[0], "w1q0")
        nc.vector.tensor_copy(sg[:], xs[:].indirect(offs_t[:]))
        for half in range(2):
            a, b = 256 * half, 256 * (half + 1)
            nc.vector.tensor_copy(xg[:, a:b], xw[:].bitcast(U32).indirect(offs_t[:, a // 16 : b // 16]))
            if half == 0:
                first_layer(0, wq0, a, b, 0)
            else:
                first_layer(0, wq0, a, a + 128, 1)
                first_layer(0, wq0, a + 128, b, 7)
        wq1 = quantised(nc.vector.tensor_copy, w1_src[1], "w1q1")
        wq2 = quantised(nc.scalar.copy, w1_src[2], "w1q2")
        wq3 = quantised(nc.scalar.copy, w1_src[3], "w1q3")
        h[1] = sb([P, S], F32, "h1", tag="w1_raw256")
        first_layer(1, wq1, 0, S, 2)
        h[2] = sb([P, S], F32, "h2")
        first_layer(2, wq2, 0, S, 0)
        h[3] = sb([P, S], F32, "h3")
        first_layer(3, wq3, 0, S, 1)

        w2g = sb([P, N, 4], BF16, "w2g")
        w2c = sb([P, N], U32, "w2c")
        w2s = sb([P, N], U8, "w2s")
        for m in range(4):
            interleave(nc.scalar.copy, w2g[:, 128 * m : 128 * (m + 1), :], w2_src[m])

        def neighbours(c, vbs, dst):
            a, b = 128 * vbs[0], 128 * (vbs[-1] + 1)
            for d in range(D):
                g = sb([P, b - a], F32, "g%d_%d_%d" % (c, a, d), tag="w1q1_g" if (c, d) == (0, 0) else None)
                nc.vector.tensor_tensor(g[:], h[c][:].indirect(pos_t[d][:, a // 16 : b // 16]), gate_t[d][:, a:b], MULT)
                for vb in vbs:
                    nc.tensor.matmul(dst[vb], lhsT=g[:, 128 * vb - a : 128 * (vb + 1) - a], rhs=ident[:],
                                     start=(d == 0), stop=(d == D - 1), is_transpose=True)

        def round_z(zt, src, p0, p1):
            nc.scalar.copy(zt[:].rearrange("v (u p e) -> v u p e", u=2, e=2)[:, :, p0:p1, :],
                           src.rearrange("v (p u e) -> v u p e", u=2, e=2))

        def turn_back(vb, zt, bk):
            back = bank(bk, [P, 2, 128], "back%d" % vb)
            words = zt[:].bitcast(F32)
            for u in range(2):
                nc.tensor.transpose(back[:, u, :], words[:, 128 * u : 128 * (u + 1)], ident[:])
            zg = sb([P, 512], BF16, "zg%d" % vb)
            nc.scalar.copy(zg[:].bitcast(F32).rearrange("p (v u) -> p v u", u=2), back[:].rearrange("p u v -> p v u"))
            return zg

        def second_layer(vb, zg, parts):
            zc = sb([P, 128], U32, "zc%d" % vb)
            zs = sb([P, 128], U8, "zs%d" % vb)
            nc.vector.quantize_mx(zc[:].bitcast(FP8X4), zs[:], zg[:])
            for m0, m1, bk, copy in parts:
                acc = bank(bk, [P, m1 - m0, 128], "out%d_%d" % (vb, m0))
                for m in range(m0, m1):
                    cols = slice(128 * m, 128 * (m + 1))
                    nc.tensor.matmul_mx(acc[:, m - m0, :], lhsT=w2c[:, cols].bitcast(FP8X4), lhsT_scale=w2s[:, cols],
                                        rhs=zc[:].bitcast(FP8X4), rhs_scale=zs[:], start=True, stop=True)
                res = sb([P, m1 - m0, 128], F32, "res%d_%d" % (vb, m0))
                rows = out[128 * m0 : 128 * m1, 128 * vb : 128 * (vb + 1)].rearrange("(j p) v -> p j v", p=P)
                copy(res[:], acc[:])
                nc.sync.dma_start(rows, res[:])

        early = [bank(3 + vb, [P, 384], "early%d" % vb) for vb in range(2)]
        for c in range(3):
            neighbours(c, [0, 1], [early[vb][:, 128 * c : 128 * (c + 1)] for vb in range(2)])
        zt0 = sb([P, H], BF16, "zt0", tag="w2_raw")
        round_z(zt0, early[0][:], 0, 96)
        zt1 = sb([P, H], BF16, "zt1")
        round_z(zt1, early[1][:], 0, 96)
        late0 = bank(5, [P, 128], "late0")
        neighbours(3, [0], {0: late0[:]})
        round_z(zt0, late0[:], 96, 128)
        late1 = bank(6, [P, 128], "late1")
        neighbours(3, [1], {1: late1[:]})
        round_z(zt1, late1[:], 96, 128)
        zg0 = turn_back(0, zt0, 2)
        zg1 = turn_back(1, zt1, 7)
        nc.vector.quantize_mx(w2c[:].bitcast(FP8X4), w2s[:], w2g[:].rearrange("p c j -> p (c j)"))
        second_layer(0, zg0, [(0, 2, 6, nc.scalar.copy), (2, 4, 3, nc.scalar.copy)])
        second_layer(1, zg1, [(0, 2, 0, nc.vector.tensor_copy), (2, 4, 1, nc.scalar.copy)])
